import numpy as np
import ml_dtypes

BF16 = ml_dtypes.bfloat16


def bf(x):
    return np.asarray(x, np.float32).astype(BF16)


def f32(x):
    return np.asarray(x, np.float32)


def f64(x):
    return np.asarray(x).astype(np.float64)


def striped(idx):
    return np.concatenate([l.reshape(-1, 16).T for l in idx])


def rows(idx, k):
    return np.tile(np.repeat(idx, 16, axis=0), (k // (16 * 8), 1))


def look(tab, idx):
    return np.take_along_axis(f64(tab), rows(idx, len(tab)), axis=1)


K, S, V, N, M = 128, 2048, 2048, 2048, 128


def setup_inputs():
    return {"tab": f32(np.random.standard_normal((2, K, S))), "x0": f32(np.random.standard_normal((K, V))), "w": bf(np.random.standard_normal((K, M)) / np.sqrt(K)), "b": f32(0.5 * np.random.standard_normal((M, 1))), "offs": striped(np.random.randint(0, S, (8, N)))}


def reference(tab, x0, w, b, offs):
    idx = np.stack([g.T.reshape(-1) for g in np.split(offs, 8)])
    x = f64(x0) * look(tab[0], idx) + look(tab[1], idx)
    y = f64(w).T @ x
    return np.maximum(y + f64(b), 0.0)

@@ -1,0 +1,52 @@
+import concourse.mybir as mybir
+
+F32, BF16, U16 = mybir.dt.float32, mybir.dt.bfloat16, mybir.dt.uint16
+ADD, MULT = mybir.AluOpType.add, mybir.AluOpType.mult
+RELU = mybir.ActivationFunctionType.Relu
+
+P = 128
+N = 2048
+PIECE = 512
+PER_COLUMN = 16
+FLOPS = 2 * P * P * N + 2 * P * N + 2 * P * N
+
+
+def tile_lookup_film_mul_relu_kernel(tc, tab, x0, w, b, offs, out):
+    nc = tc.nc
+    with (
+        tc.tile_pool(name="held", bufs=1) as held,
+        tc.tile_pool(name="work", bufs=N // PIECE) as work,
+        tc.psum_pool(name="psum", bufs=N // PIECE) as psum,
+    ):
+        offsets = held.tile([P, N // PER_COLUMN], U16, name="offsets")
+        nc.sync.dma_start(offsets[:], offs)
+        gains = held.tile([P, N], F32, name="gains")
+        nc.sync.dma_start(gains[:], tab[0])
+        features = [held.tile([P, PIECE], F32, name=f"features{c}") for c in range(N // PIECE)]
+        for c in range(N // PIECE):
+            nc.sync.dma_start(features[c][:], x0[:, c * PIECE : (c + 1) * PIECE])
+        shifts = held.tile([P, N], F32, name="shifts")
+        nc.sync.dma_start(shifts[:], tab[1])
+        weights = held.tile([P, P], BF16, name="weights")
+        nc.scalar.dma_start(weights[:], w)
+        bias = held.tile([P, 1], F32, name="bias")
+        nc.scalar.dma_start(bias[:], b)
+
+        def listed(table, c):
+            first = c * PIECE // PER_COLUMN
+            return table[:].indirect(offsets[:, first : first + PIECE // PER_COLUMN])
+
+        scaled = [held.tile([P, PIECE], F32, name=f"scaled{c}") for c in range(N // PIECE)]
+        for c in range(N // PIECE):
+            nc.vector.tensor_tensor(scaled[c][:], listed(gains, c), features[c][:], MULT)
+
+        for c in range(N // PIECE):
+            x = work.tile([P, PIECE], F32, name="x")
+            nc.vector.tensor_tensor(x[:], listed(shifts, c), scaled[c][:], ADD)
+            x_rounded = work.tile([P, PIECE], BF16, name="x_rounded")
+            nc.scalar.copy(x_rounded[:], x[:])
+            y = psum.tile([P, PIECE], F32, name="y")
+            nc.tensor.matmul(y[:], weights[:], x_rounded[:], start=True, stop=True)
+            result = work.tile([P, PIECE], F32, name="result")
+            nc.scalar.activation(result[:], y[:], RELU, bias=bias[:])
+            nc.sync.dma_start(out[:, c * PIECE : (c + 1) * PIECE], result[:])

@@ -1,12 +1,15 @@
 import concourse.mybir as mybir
 
 F32, BF16, U16 = mybir.dt.float32, mybir.dt.bfloat16, mybir.dt.uint16
-ADD, MULT = mybir.AluOpType.add, mybir.AluOpType.mult
+ADD, MULT, MAX = mybir.AluOpType.add, mybir.AluOpType.mult, mybir.AluOpType.max
 RELU = mybir.ActivationFunctionType.Relu
 
 P = 128
 N = 2048
 PIECE = 512
+PIECES = N // PIECE
+HALF = PIECE // 2
+LEAD = 2
 PER_COLUMN = 16
 FLOPS = 2 * P * P * N + 2 * P * N + 2 * P * N
 
@@ -15,18 +18,19 @@ def tile_lookup_film_mul_relu_kernel(tc, tab, x0, w, b, offs, out):
     nc = tc.nc
     with (
         tc.tile_pool(name="held", bufs=1) as held,
-        tc.tile_pool(name="work", bufs=N // PIECE) as work,
-        tc.psum_pool(name="psum", bufs=N // PIECE) as psum,
+        tc.tile_pool(name="work", bufs=PIECES) as work,
+        tc.psum_pool(name="psum", bufs=PIECES + 1) as psum,
     ):
         offsets = held.tile([P, N // PER_COLUMN], U16, name="offsets")
         nc.sync.dma_start(offsets[:], offs)
         gains = held.tile([P, N], F32, name="gains")
         nc.sync.dma_start(gains[:], tab[0])
-        features = [held.tile([P, PIECE], F32, name=f"features{c}") for c in range(N // PIECE)]
-        for c in range(N // PIECE):
-            nc.sync.dma_start(features[c][:], x0[:, c * PIECE : (c + 1) * PIECE])
+        features = [held.tile([P, PIECE], F32, name=f"features{c}") for c in range(PIECES)]
         shifts = held.tile([P, N], F32, name="shifts")
-        nc.sync.dma_start(shifts[:], tab[1])
+        for c in range(PIECES):
+            if c == LEAD + 1:
+                nc.sync.dma_start(shifts[:], tab[1])
+            nc.sync.dma_start(features[c][:], x0[:, c * PIECE : (c + 1) * PIECE])
         weights = held.tile([P, P], BF16, name="weights")
         nc.scalar.dma_start(weights[:], w)
         bias = held.tile([P, 1], F32, name="bias")
@@ -36,13 +40,17 @@ def tile_lookup_film_mul_relu_kernel(tc, tab, x0, w, b, offs, out):
             first = c * PIECE // PER_COLUMN
             return table[:].indirect(offsets[:, first : first + PIECE // PER_COLUMN])
 
-        scaled = [held.tile([P, PIECE], F32, name=f"scaled{c}") for c in range(N // PIECE)]
-        for c in range(N // PIECE):
-            nc.vector.tensor_tensor(scaled[c][:], listed(gains, c), features[c][:], MULT)
+        def product(c):
+            scaled = work.tile([P, PIECE], F32, name="scaled")
+            nc.vector.tensor_tensor(scaled[:], listed(gains, c), features[c][:], MULT)
+            return scaled
 
-        for c in range(N // PIECE):
+        def modulated(c, scaled):
             x = work.tile([P, PIECE], F32, name="x")
-            nc.vector.tensor_tensor(x[:], listed(shifts, c), scaled[c][:], ADD)
+            nc.vector.tensor_tensor(x[:], listed(shifts, c), scaled[:], ADD)
+            return x
+
+        def layer_by_scalar(c, x):
             x_rounded = work.tile([P, PIECE], BF16, name="x_rounded")
             nc.scalar.copy(x_rounded[:], x[:])
             y = psum.tile([P, PIECE], F32, name="y")
@@ -50,3 +58,31 @@ def tile_lookup_film_mul_relu_kernel(tc, tab, x0, w, b, offs, out):
             result = work.tile([P, PIECE], F32, name="result")
             nc.scalar.activation(result[:], y[:], RELU, bias=bias[:])
             nc.sync.dma_start(out[:, c * PIECE : (c + 1) * PIECE], result[:])
+
+        def layer_by_both(c, x):
+            banks = []
+            for h in range(2):
+                half_rounded = work.tile([P, HALF], BF16, name="half_rounded")
+                nc.vector.tensor_copy(half_rounded[:], x[:, h * HALF : (h + 1) * HALF])
+                y = psum.tile([P, PIECE], F32, name="y")
+                nc.tensor.matmul(y[:, :HALF], weights[:], half_rounded[:], start=True, stop=True)
+                banks.append(y)
+            first, second = c * PIECE, c * PIECE + HALF
+            by_vector = work.tile([P, HALF], F32, name="by_vector")
+            nc.vector.tensor_scalar(by_vector[:], banks[0][:, :HALF], bias[:], 0.0, ADD, MAX)
+            nc.sync.dma_start(out[:, first : first + HALF], by_vector[:])
+            by_scalar = work.tile([P, HALF], F32, name="by_scalar")
+            nc.scalar.activation(by_scalar[:], banks[1][:, :HALF], RELU, bias=bias[:])
+            nc.scalar.dma_start(out[:, second : second + HALF], by_scalar[:])
+
+        products = []
+        for step in range(PIECES + LEAD):
+            if step < PIECES:
+                products.append(product(step))
+            c = step - LEAD
+            if c >= 0:
+                x = modulated(c, products[c])
+                if c < PIECES - 1:
+                    layer_by_scalar(c, x)
+                else:
+                    layer_by_both(c, x)

@@ -32,9 +32,9 @@ def tile_lookup_film_mul_relu_kernel(tc, tab, x0, w, b, offs, out):
                 nc.sync.dma_start(shifts[:], tab[1])
             nc.sync.dma_start(features[c][:], x0[:, c * PIECE : (c + 1) * PIECE])
         weights = held.tile([P, P], BF16, name="weights")
-        nc.scalar.dma_start(weights[:], w)
+        nc.sync.dma_start(weights[:], w)
         bias = held.tile([P, 1], F32, name="bias")
-        nc.scalar.dma_start(bias[:], b)
+        nc.sync.dma_start(bias[:], b)
 
         def listed(table, c):
             first = c * PIECE // PER_COLUMN

@@ -9,7 +9,8 @@ N = 2048
 PIECE = 512
 PIECES = N // PIECE
 HALF = PIECE // 2
-LEAD = 2
+STARTS = (0, HALF, HALF + PIECE, HALF + 2 * PIECE)
+PRODUCTS = tuple(zip(STARTS, STARTS[1:] + (N,)))
 PER_COLUMN = 16
 FLOPS = 2 * P * P * N + 2 * P * N + 2 * P * N
 
@@ -25,30 +26,18 @@ def tile_lookup_film_mul_relu_kernel(tc, tab, x0, w, b, offs, out):
         nc.sync.dma_start(offsets[:], offs)
         gains = held.tile([P, N], F32, name="gains")
         nc.sync.dma_start(gains[:], tab[0])
-        features = [held.tile([P, PIECE], F32, name=f"features{c}") for c in range(PIECES)]
+        features = held.tile([P, N], F32, name="features")
+        for a, z in PRODUCTS:
+            nc.sync.dma_start(features[:, a:z], x0[:, a:z])
         shifts = held.tile([P, N], F32, name="shifts")
-        for c in range(PIECES):
-            if c == LEAD + 1:
-                nc.sync.dma_start(shifts[:], tab[1])
-            nc.sync.dma_start(features[c][:], x0[:, c * PIECE : (c + 1) * PIECE])
+        nc.sync.dma_start(shifts[:], tab[1])
         weights = held.tile([P, P], BF16, name="weights")
         nc.sync.dma_start(weights[:], w)
         bias = held.tile([P, 1], F32, name="bias")
         nc.sync.dma_start(bias[:], b)
 
-        def listed(table, c):
-            first = c * PIECE // PER_COLUMN
-            return table[:].indirect(offsets[:, first : first + PIECE // PER_COLUMN])
-
-        def product(c):
-            scaled = work.tile([P, PIECE], F32, name="scaled")
-            nc.vector.tensor_tensor(scaled[:], listed(gains, c), features[c][:], MULT)
-            return scaled
-
-        def modulated(c, scaled):
-            x = work.tile([P, PIECE], F32, name="x")
-            nc.vector.tensor_tensor(x[:], listed(shifts, c), scaled[:], ADD)
-            return x
+        def listed(table, a, z):
+            return table[:].indirect(offsets[:, a // PER_COLUMN : z // PER_COLUMN])
 
         def layer_by_scalar(c, x):
             x_rounded = work.tile([P, PIECE], BF16, name="x_rounded")
@@ -75,14 +64,15 @@ def tile_lookup_film_mul_relu_kernel(tc, tab, x0, w, b, offs, out):
             nc.scalar.activation(by_scalar[:], banks[1][:, :HALF], RELU, bias=bias[:])
             nc.scalar.dma_start(out[:, second : second + HALF], by_scalar[:])
 
-        products = []
-        for step in range(PIECES + LEAD):
-            if step < PIECES:
-                products.append(product(step))
-            c = step - LEAD
-            if c >= 0:
-                x = modulated(c, products[c])
-                if c < PIECES - 1:
-                    layer_by_scalar(c, x)
-                else:
-                    layer_by_both(c, x)
+        scaled = held.tile([P, N], F32, name="scaled")
+        for a, z in PRODUCTS:
+            nc.vector.tensor_tensor(scaled[:, a:z], listed(gains, a, z), features[:, a:z], MULT)
+
+        for c in range(PIECES):
+            a, z = c * PIECE, (c + 1) * PIECE
+            x = work.tile([P, PIECE], F32, name="x")
+            nc.vector.tensor_tensor(x[:], listed(shifts, a, z), scaled[:, a:z], ADD)
+            if c < PIECES - 1:
+                layer_by_scalar(c, x)
+            else:
+                layer_by_both(c, x)

import concourse.mybir as mybir

F32, BF16, U16 = mybir.dt.float32, mybir.dt.bfloat16, mybir.dt.uint16
ADD, MULT, MAX = mybir.AluOpType.add, mybir.AluOpType.mult, mybir.AluOpType.max
RELU = mybir.ActivationFunctionType.Relu

P = 128
N = 2048
PIECE = 512
PIECES = N // PIECE
HALF = PIECE // 2
STARTS = (0, HALF, HALF + PIECE, HALF + 2 * PIECE)
PRODUCTS = tuple(zip(STARTS, STARTS[1:] + (N,)))
PER_COLUMN = 16
FLOPS = 2 * P * P * N + 2 * P * N + 2 * P * N


def tile_lookup_film_mul_relu_kernel(tc, tab, x0, w, b, offs, out):
    nc = tc.nc
    with (
        tc.tile_pool(name="held", bufs=1) as held,
        tc.tile_pool(name="work", bufs=PIECES) as work,
        tc.psum_pool(name="psum", bufs=PIECES + 1) as psum,
    ):
        offsets = held.tile([P, N // PER_COLUMN], U16, name="offsets")
        nc.sync.dma_start(offsets[:], offs)
        gains = held.tile([P, N], F32, name="gains")
        nc.sync.dma_start(gains[:], tab[0])
        features = held.tile([P, N], F32, name="features")
        for a, z in PRODUCTS:
            nc.sync.dma_start(features[:, a:z], x0[:, a:z])
        shifts = held.tile([P, N], F32, name="shifts")
        nc.sync.dma_start(shifts[:], tab[1])
        weights = held.tile([P, P], BF16, name="weights")
        nc.sync.dma_start(weights[:], w)
        bias = held.tile([P, 1], F32, name="bias")
        nc.sync.dma_start(bias[:], b)

        def listed(table, a, z):
            return table[:].indirect(offsets[:, a // PER_COLUMN : z // PER_COLUMN])

        def layer_by_scalar(c, x):
            x_rounded = work.tile([P, PIECE], BF16, name="x_rounded")
            nc.scalar.copy(x_rounded[:], x[:])
            y = psum.tile([P, PIECE], F32, name="y")
            nc.tensor.matmul(y[:], weights[:], x_rounded[:], start=True, stop=True)
            result = work.tile([P, PIECE], F32, name="result")
            nc.scalar.activation(result[:], y[:], RELU, bias=bias[:])
            nc.sync.dma_start(out[:, c * PIECE : (c + 1) * PIECE], result[:])

        def layer_by_both(c, x):
            banks = []
            for h in range(2):
                half_rounded = work.tile([P, HALF], BF16, name="half_rounded")
                nc.vector.tensor_copy(half_rounded[:], x[:, h * HALF : (h + 1) * HALF])
                y = psum.tile([P, PIECE], F32, name="y")
                nc.tensor.matmul(y[:, :HALF], weights[:], half_rounded[:], start=True, stop=True)
                banks.append(y)
            first, second = c * PIECE, c * PIECE + HALF
            by_vector = work.tile([P, HALF], F32, name="by_vector")
            nc.vector.tensor_scalar(by_vector[:], banks[0][:, :HALF], bias[:], 0.0, ADD, MAX)
            nc.sync.dma_start(out[:, first : first + HALF], by_vector[:])
            by_scalar = work.tile([P, HALF], F32, name="by_scalar")
            nc.scalar.activation(by_scalar[:], banks[1][:, :HALF], RELU, bias=bias[:])
            nc.scalar.dma_start(out[:, second : second + HALF], by_scalar[:])

        scaled = held.tile([P, N], F32, name="scaled")
        for a, z in PRODUCTS:
            nc.vector.tensor_tensor(scaled[:, a:z], listed(gains, a, z), features[:, a:z], MULT)

        for c in range(PIECES):
            a, z = c * PIECE, (c + 1) * PIECE
            x = work.tile([P, PIECE], F32, name="x")
            nc.vector.tensor_tensor(x[:], listed(shifts, a, z), scaled[:, a:z], ADD)
            if c < PIECES - 1:
                layer_by_scalar(c, x)
            else:
                layer_by_both(c, x)
